import numpy as np
import ml_dtypes


def mxq(x, axis, fmt="e4m3"):
    dtype, down = {"e4m3": (ml_dtypes.float8_e4m3fn, 7), "e5m2": (ml_dtypes.float8_e5m2, 14)}[fmt]
    v = np.moveaxis(np.asarray(x, np.float32).astype(ml_dtypes.bfloat16).astype(np.float64), axis, -1)
    blocks = v.reshape(v.shape[:-1] + (-1, 32))
    amax = np.abs(blocks).max(-1, keepdims=True)
    byte = np.maximum(np.where(amax > 0, np.frexp(amax)[1] - 1 + 127, 0) - down, 1)
    scale = np.exp2(byte - 127.0)
    codes = (blocks / scale).astype(np.float32).astype(dtype).astype(np.float64)
    return np.moveaxis((codes * scale).reshape(v.shape), -1, axis)


WIDE = False


def mx_kscale(k):
    if not WIDE:
        return np.ones(k)
    levels = np.array([10, -10, 5, -5, 0])
    if k % 512:
        return np.exp2(np.random.permutation(np.resize(levels, k // 32))).repeat(32)
    a = np.empty((k // 512, 16))
    for p in range(k // 512):
        a[p, :8] = np.random.permutation(np.resize(levels, 8))
        for g in range(8):
            far = levels[np.abs(levels - a[p, g]) >= 10]
            a[p, g + 8] = far[np.random.randint(len(far))]
    return np.exp2(a.ravel()).repeat(32)


def f64(x):
    return np.asarray(x).astype(np.float64)


def striped(idx):
    return np.tile(idx.reshape(-1, 16).T, (8, 1)).astype(np.uint16)


def unstriped(offs):
    return offs[:16].T.reshape(-1).astype(np.int64)


E2M1 = np.array([0.0, 0.5, 1.0, 1.5, 2.0, 3.0, 4.0, 6.0, -0.0, -0.5, -1.0, -1.5, -2.0, -3.0, -4.0, -6.0])


def pack_weight(w, fmt):
    k, n = w.shape
    w = f64(np.asarray(w, np.float32).astype(ml_dtypes.bfloat16)).reshape(k // 32, 32, n)
    amax = np.abs(w).max(1)
    if fmt == "e4m3":
        byte = np.frexp(amax)[1] - 1 + 127 - 7
    else:
        mant, ex = np.frexp(amax / 6.0)
        byte = np.where(mant > 0.5, ex, ex - 1) + 127
    byte = np.clip(np.where(amax > 0, byte, 1), 1, 254)
    scaled = (w * np.exp2(127.0 - byte)[:, None, :]).reshape(k, n).astype(np.float32)
    by_word = np.ascontiguousarray(scaled.reshape(k // 512, 128, 4, n).transpose(0, 1, 3, 2))
    if fmt == "e4m3":
        words = by_word.astype(ml_dtypes.float8_e4m3fn).view(np.uint8)
    else:
        c = by_word.astype(ml_dtypes.float4_e2m1fn).view(np.uint8) & 0xF
        words = (c[..., 0::2] | (c[..., 1::2] << 4)).reshape(k // 512, 128, 2 * n)
    return np.ascontiguousarray(words), np.ascontiguousarray(byte.astype(np.uint8).reshape(k // 512, 16, n))


def unpack_weight(words, scales, fmt):
    g, _, n = scales.shape
    words = np.ascontiguousarray(words).reshape(g, 128, n, -1)
    if fmt == "e4m3":
        vals = words.view(ml_dtypes.float8_e4m3fn).astype(np.float64)
    else:
        nib = np.empty((g, 128, n, 4), np.uint8)
        nib[..., 0::2] = words & 0xF
        nib[..., 1::2] = words >> 4
        vals = E2M1[nib]
    vals = vals * np.repeat(np.exp2(scales.astype(np.float64) - 127.0), 8, axis=1)[..., None]
    return vals.transpose(0, 1, 3, 2).reshape(g * 512, n)


def silu(v):
    return v / (1.0 + np.exp(-np.maximum(v, -700.0)))


K, T, E, C, H, N = 1536, 640, 4, 256, 512, 384
PAD = 32


def by_expert(wq, xq):
    return np.concatenate([wq[e].T @ xq[:, e * C:(e + 1) * C] for e in range(E)], axis=1)


def setup_inputs():
    n = np.random.standard_normal
    s = mx_kscale(K)[:, None]
    u = mx_kscale(H)
    first = np.random.permutation(np.repeat(np.arange(E), T // E))
    second = (first + 1 + np.random.permutation(np.repeat(np.arange(E - 1), -(-T // (E - 1)))[:T])) % E
    while np.bincount(second, minlength=E).max() != T // E:
        load = np.bincount(second, minlength=E); hi, lo = int(load.argmax()), int(load.argmin())
        t = np.flatnonzero((second == hi) & (first != lo))[0]; second[t] = lo
    slot_token = np.empty(E * C, np.int64); pos = np.empty((2, T), np.int64); fill = np.zeros(E, np.int64)
    place = np.stack([np.random.permutation(C) for _ in range(E)])
    for r, deal in enumerate((first, second)):
        for t in np.random.permutation(T):
            e = deal[t]
            if fill[e] < C: j = e * C + place[e, fill[e]]; fill[e] += 1; slot_token[j] = t; pos[r, t] = j
            else: pos[r, t] = E * C + t % PAD
    g = np.random.uniform(0.2, 0.8, T)
    w1 = [pack_weight(m, "e2m1") for m in n((E, K, H)) / np.sqrt(K) / s[None] * u[None, None, :]]
    w2 = [pack_weight(m, "e2m1") for m in n((E, H, N)) / np.sqrt(H) / u[None, :, None]]
    return {
        "xT": (n((K, T)) * s).astype(np.float32),
        "w1_words": np.stack([m[0] for m in w1]),
        "w1_scales": np.stack([m[1] for m in w1]),
        "w2_words": np.stack([m[0] for m in w2]),
        "w2_scales": np.stack([m[1] for m in w2]),
        "gate": np.stack([np.tile(g, (N, 1)), np.tile(1.0 - g, (N, 1))]).astype(np.float32),
        "offs": striped(slot_token),
        "pos1": striped(pos[0]),
        "pos2": striped(pos[1]),
    }


def reference(xT, w1_words, w1_scales, w2_words, w2_scales, gate, offs, pos1, pos2):
    idx = unstriped(offs)
    w1 = np.stack([unpack_weight(w1_words[e], w1_scales[e], "e2m1") for e in range(E)])
    w2 = np.stack([unpack_weight(w2_words[e], w2_scales[e], "e2m1") for e in range(E)])
    xq = mxq(f64(xT)[:, idx], 0, "e4m3")
    h = silu(by_expert(w1, xq))
    y = by_expert(w2, mxq(h, 0, "e4m3"))
    y = np.concatenate([y, np.zeros((N, PAD))], axis=1)
    return f64(gate[0]) * y[:, unstriped(pos1)] + f64(gate[1]) * y[:, unstriped(pos2)]

@@ -1,0 +1,242 @@
+from contextlib import ExitStack
+
+import concourse.mybir as mybir
+from concourse.masks import make_identity
+
+K, T, E, C, H, N = 1536, 640, 4, 256, 512, 384
+PAD = 32
+S = E * C
+PASSES = K // 512
+NB = N // 128
+
+FLOPS = 2 * S * H * (K + N)
+BYTES = 4 * K * T + E * K * H // 2 + E * K * H // 32 + E * H * N // 2 + E * H * N // 32 + 2 * 4 * T + 2 * (S + 2 * T) + 4 * N * T
+
+F32 = mybir.dt.float32
+BF16 = mybir.dt.bfloat16
+U32 = mybir.dt.uint32
+I32 = mybir.dt.int32
+U16 = mybir.dt.uint16
+U8 = mybir.dt.uint8
+FP8X4 = mybir.dt.float8_e4m3fn_x4
+FP4X4 = mybir.dt.float4_e2m1fn_x4
+COPY = mybir.ActivationFunctionType.Copy
+SILU = mybir.ActivationFunctionType.Silu
+MULT = mybir.AluOpType.mult
+ADD = mybir.AluOpType.add
+
+UNITS = [(0, 256), (256, 256), (512, 256), (768, 128), (896, 128)]
+CUTS = [(0, 384), (384, 384), (768, 256)]
+
+
+def tile_moe_cap2_mlp_silu_kernel(tc, xT, w1_words, w1_scales, w2_words, w2_scales, gate, offs, pos1, pos2, out):
+    nc = tc.nc
+    with ExitStack() as ctx:
+        lists = ctx.enter_context(tc.tile_pool(name="lists", bufs=1))
+        keep = ctx.enter_context(tc.tile_pool(name="keep", bufs=1))
+        pacc = ctx.enter_context(tc.psum_pool(name="pacc", bufs=4))
+        ptr = ctx.enter_context(tc.psum_pool(name="ptr", bufs=2))
+        py = ctx.enter_context(tc.psum_pool(name="py", bufs=2))
+
+        offs_t = lists.tile([128, S // 16], U16, name="offs_t")
+        pos1_t = lists.tile([128, T // 16], U16, name="pos1_t")
+        pos2_t = lists.tile([128, T // 16], U16, name="pos2_t")
+
+        chunks = {0: [(0, 256), (256, 384)], 1: [(0, 640)], 2: [(0, 640)]}
+        quant = {0: [(0, 256), (256, 256), (512, 128)], 1: [(0, 512), (512, 128)], 2: [(0, 512), (512, 128)]}
+
+        raw = {}
+        for s in range(PASSES):
+            rows = xT[512 * s : 512 * (s + 1), :].rearrange("(p j) t -> p j t", j=4)
+            for lo, w in chunks[s]:
+                r = keep.tile([128, 4, w], F32, name=f"raw_{s}_{lo}")
+                nc.sync.dma_start(r[:], rows[:, :, lo : lo + w])
+                raw[s, lo] = r
+            if s == 0:
+                nc.sync.dma_start(offs_t[:], offs)
+
+        warm = keep.tile([128, 1], F32, name="warm")
+        warm_out = keep.tile([128, 1], F32, name="warm_out")
+        nc.vector.memset(warm[:], 0.0)
+        nc.scalar.activation(warm_out[:], warm[:], SILU)
+
+        tok_scales = []
+        for s in range(PASSES):
+            z = keep.tile([128, T], U8, name=f"tok_scales_{s}", align_bytes=64)
+            nc.gpsimd.memset(z[:], 0)
+            tok_scales.append(z)
+        w1s = keep.tile([128, E * PASSES * H], U8, name="w1s", align_bytes=64)
+        w2s = keep.tile([128, E * N], U8, name="w2s", align_bytes=64)
+        nc.vector.memset(w1s[:].bitcast(I32), 0)
+        nc.vector.memset(w2s[:].bitcast(I32), 0)
+        ident = keep.tile([128, 128], F32, name="ident")
+        make_identity(nc, ident[:])
+        y = []
+        for b in range(NB):
+            yb = keep.tile([128, S + PAD], F32, name=f"y_{b}", align_bytes=64)
+            nc.vector.memset(yb[:, S:], 0.0)
+            y.append(yb)
+
+        for Q in range(4):
+            nc.sync.dma_start(
+                w1s[32 * Q : 32 * Q + 4, :].bitcast(I32).rearrange("p (g i) -> p g i", g=E * PASSES),
+                w1_scales[:, :, 4 * Q : 4 * Q + 4, :].bitcast(I32).rearrange("e s q i -> q (e s) i"),
+            )
+        for Q in range(4):
+            nc.sync.dma_start(
+                w2s[32 * Q : 32 * Q + 4, :].bitcast(I32).rearrange("p (g i) -> p g i", g=E),
+                w2_scales[:, 0, 4 * Q : 4 * Q + 4, :].bitcast(I32).rearrange("e q i -> q e i"),
+            )
+        w1w = []
+        for e in range(E):
+            w = keep.tile([128, PASSES * 2 * H], U8, name=f"w1w_{e}", align_bytes=64)
+            nc.sync.dma_start(
+                w[:].bitcast(I32).rearrange("p (s i) -> p s i", s=PASSES),
+                w1_words[e].bitcast(I32).rearrange("s p i -> p s i"),
+            )
+            w1w.append(w)
+        w2w = keep.tile([128, E * 2 * N], U8, name="w2w", align_bytes=64)
+        nc.sync.dma_start(
+            w2w[:].bitcast(I32).rearrange("p (e i) -> p e i", e=E),
+            w2_words[:, 0].bitcast(I32).rearrange("e p i -> p e i"),
+        )
+        nc.sync.dma_start(pos1_t[:], pos1)
+        nc.sync.dma_start(pos2_t[:], pos2)
+        gates = []
+        for r in range(2):
+            g = keep.tile([128, T], F32, name=f"gate_{r}")
+            nc.sync.dma_start(g[:], gate[r, 0:128, :])
+            gates.append(g)
+
+        codes, slot_codes, slot_scales = [], [], []
+        for s in range(PASSES):
+            c = keep.tile([128, T], U32, name=f"tok_codes_{s}", align_bytes=64)
+            sc = keep.tile([128, S], U32, name=f"slot_codes_{s}", align_bytes=64)
+            ss = keep.tile([128, S], U8, name=f"slot_scales_{s}", align_bytes=64)
+            codes.append(c)
+            slot_codes.append(sc)
+            slot_scales.append(ss)
+
+        def cast(engine, s, lo, w, a, b, grouped):
+            dst = grouped[:, 4 * a : 4 * b].rearrange("p (c i t) -> p c t i", i=4, t=4)
+            src = raw[s, lo][:, :, a - lo : b - lo].rearrange("p t (c i) -> p c t i", i=4)
+            if engine == "v":
+                nc.vector.tensor_copy(dst, src)
+            else:
+                nc.scalar.activation(dst, src, COPY)
+
+        def load_pass(s):
+            grouped = keep.tile([128, 4 * T], BF16, name=f"grouped_{s}", align_bytes=64)
+            if s == 0:
+                cast("s", 0, 0, 256, 0, 96, grouped)
+                cast("v", 0, 0, 256, 96, 256, grouped)
+                cast("s", 0, 256, 384, 256, 384, grouped)
+                cast("v", 0, 256, 384, 384, 640, grouped)
+            else:
+                cast("s", s, 0, 640, 0, 320, grouped)
+                cast("s", s, 0, 640, 320, 640, grouped)
+            for lo, w in quant[s]:
+                nc.vector.quantize_mx(
+                    out=codes[s][:, lo : lo + w].bitcast(FP8X4),
+                    scales=tok_scales[s][:, lo : lo + w],
+                    in_=grouped[:, 4 * lo : 4 * (lo + w)],
+                )
+
+        def gather(s, lo, w):
+            ids = offs_t[:, lo // 16 : (lo + w) // 16]
+            nc.vector.tensor_copy(slot_codes[s][:, lo : lo + w], codes[s][:].indirect(ids))
+            nc.vector.tensor_copy(slot_scales[s][:, lo : lo + w], tok_scales[s][:].indirect(ids))
+
+        def layer1(m):
+            e = m // 2
+            cols = slice(128 * m, 128 * (m + 1))
+            acc = pacc.tile([128, H], F32, name="acc")
+            for s in range(PASSES):
+                nc.tensor.matmul_mx(
+                    out=acc[:],
+                    lhsT=slot_codes[s][:, cols].bitcast(FP8X4),
+                    lhsT_scale=slot_scales[s][:, cols],
+                    rhs=w1w[e][:, 2 * H * s : 2 * H * (s + 1)].bitcast(FP4X4),
+                    rhs_scale=w1s[:, H * (PASSES * e + s) : H * (PASSES * e + s + 1)],
+                    start=(s == 0),
+                    stop=(s == PASSES - 1),
+                )
+            h = keep.tile([128, H], BF16, name=f"h_{m}", align_bytes=64)
+            nc.scalar.activation(
+                h[:].rearrange("p (u q d) -> p u q d", u=2, d=2),
+                acc[:].rearrange("p (q u d) -> p u q d", u=2, d=2),
+                SILU,
+            )
+            return h
+
+        def turn(h, hg, at):
+            words = h[:].bitcast(F32)
+            tp = ptr.tile([128, 2, 128], F32, name="tp")
+            for u in range(2):
+                nc.tensor.transpose(tp[:, u, :], words[:, 128 * u : 128 * (u + 1)], ident[:])
+            nc.scalar.copy(
+                hg[:, 4 * at : 4 * (at + 128)].bitcast(F32).rearrange("p (r u) -> p r u", u=2),
+                tp[:].rearrange("p u r -> p r u"),
+            )
+
+        def layer2(unit, hg):
+            lo, w = unit
+            e = lo // C
+            hc = keep.tile([128, w], U32, name=f"hc_{lo}", align_bytes=64)
+            hs = keep.tile([128, w], U8, name=f"hs_{lo}", align_bytes=64)
+            nc.vector.quantize_mx(out=hc[:].bitcast(FP8X4), scales=hs[:], in_=hg[:])
+            for b in range(NB):
+                p = py.tile([128, w], F32, name="p")
+                nc.tensor.matmul_mx(
+                    out=p[:],
+                    lhsT=w2w[:, 2 * (N * e + 128 * b) : 2 * (N * e + 128 * (b + 1))].bitcast(FP4X4),
+                    lhsT_scale=w2s[:, N * e + 128 * b : N * e + 128 * (b + 1)],
+                    rhs=hc[:].bitcast(FP8X4),
+                    rhs_scale=hs[:],
+                    start=True,
+                    stop=True,
+                )
+                nc.scalar.copy(y[b][:, lo : lo + w], p[:])
+
+        for s in range(PASSES - 1):
+            load_pass(s)
+            for lo, w in CUTS:
+                gather(s, lo, w)
+        load_pass(PASSES - 1)
+
+        pending = None
+        for unit in UNITS:
+            lo, w = unit
+            gather(PASSES - 1, lo, w)
+            hg = keep.tile([128, 4 * w], BF16, name=f"hg_{lo}", align_bytes=64)
+            hs_ = [layer1(m) for m in range(lo // 128, (lo + w) // 128)]
+            if pending is not None:
+                layer2(*pending)
+            for i, h in enumerate(hs_):
+                turn(h, hg, 128 * i)
+            pending = (unit, hg)
+        layer2(*pending)
+
+        prods = {}
+        outs = {}
+
+        def product(b, r):
+            t = keep.tile([128, T], F32, name=f"prod_{b}_{r}")
+            ids = (pos1_t, pos2_t)[r]
+            nc.vector.tensor_tensor(t[:], y[b][:].indirect(ids[:]), gates[r][:], MULT)
+            prods[b, r] = t
+
+        def total(b):
+            o = keep.tile([128, T], F32, name=f"o_{b}")
+            nc.vector.tensor_tensor(o[:], prods[b, 0][:], prods[b, 1][:], ADD)
+            nc.sync.dma_start(out[128 * b : 128 * (b + 1), :], o[:])
+
+        product(0, 0)
+        product(0, 1)
+        product(1, 0)
+        total(0)
+        product(1, 1)
+        product(2, 0)
+        total(1)
+        product(2, 1)
+        total(2)

@@ -25,8 +25,16 @@ SILU = mybir.ActivationFunctionType.Silu
 MULT = mybir.AluOpType.mult
 ADD = mybir.AluOpType.add
 
+CHUNKS = [(0, 384), (384, 256)]
+CASTS = [
+    [(0, 160, "s"), (160, 224, "v"), (384, 96, "s"), (480, 160, "v")],
+    [(0, 384, "s"), (384, 160, "s"), (544, 96, "v")],
+    [(0, 384, "s"), (384, 256, "s")],
+]
 UNITS = [(0, 256), (256, 256), (512, 256), (768, 128), (896, 128)]
-CUTS = [(0, 384), (384, 384), (768, 256)]
+QUANT = [(0, 256), (256, 128), (384, 256)]
+TURN = "ssssvvvv"
+YCOPY = {(0, 1): "v", (256, 1): "v", (512, 1): "v", (768, 1): "v"}
 
 
 def tile_moe_cap2_mlp_silu_kernel(tc, xT, w1_words, w1_scales, w2_words, w2_scales, gate, offs, pos1, pos2, out):
@@ -34,22 +42,21 @@ def tile_moe_cap2_mlp_silu_kernel(tc, xT, w1_words, w1_scales, w2_words, w2_scal
     with ExitStack() as ctx:
         lists = ctx.enter_context(tc.tile_pool(name="lists", bufs=1))
         keep = ctx.enter_context(tc.tile_pool(name="keep", bufs=1))
-        pacc = ctx.enter_context(tc.psum_pool(name="pacc", bufs=4))
+        turns = ctx.enter_context(tc.tile_pool(name="turns", bufs=1))
+        pacc = ctx.enter_context(tc.psum_pool(name="pacc", bufs=3))
         ptr = ctx.enter_context(tc.psum_pool(name="ptr", bufs=2))
-        py = ctx.enter_context(tc.psum_pool(name="py", bufs=2))
+        py = ctx.enter_context(tc.psum_pool(name="py", bufs=3))
 
         offs_t = lists.tile([128, S // 16], U16, name="offs_t")
         pos1_t = lists.tile([128, T // 16], U16, name="pos1_t")
         pos2_t = lists.tile([128, T // 16], U16, name="pos2_t")
 
-        chunks = {0: [(0, 256), (256, 384)], 1: [(0, 640)], 2: [(0, 640)]}
-        quant = {0: [(0, 256), (256, 256), (512, 128)], 1: [(0, 512), (512, 128)], 2: [(0, 512), (512, 128)]}
-
         raw = {}
         for s in range(PASSES):
             rows = xT[512 * s : 512 * (s + 1), :].rearrange("(p j) t -> p j t", j=4)
-            for lo, w in chunks[s]:
-                r = keep.tile([128, 4, w], F32, name=f"raw_{s}_{lo}")
+            for lo, w in CHUNKS:
+                pool = turns if s == 2 else keep
+                r = pool.tile([128, 4, w], F32, name=f"raw_{s}_{lo}", tag=f"raw_{s}_{lo}", align_bytes=64)
                 nc.sync.dma_start(r[:], rows[:, :, lo : lo + w])
                 raw[s, lo] = r
             if s == 0:
@@ -61,14 +68,14 @@ def tile_moe_cap2_mlp_silu_kernel(tc, xT, w1_words, w1_scales, w2_words, w2_scal
         nc.scalar.activation(warm_out[:], warm[:], SILU)
 
         tok_scales = []
-        for s in range(PASSES):
+        for s in range(2):
             z = keep.tile([128, T], U8, name=f"tok_scales_{s}", align_bytes=64)
             nc.gpsimd.memset(z[:], 0)
             tok_scales.append(z)
+        moved = keep.tile([128, S], U8, name="moved", align_bytes=64)
+        nc.gpsimd.memset(moved[:], 0)
         w1s = keep.tile([128, E * PASSES * H], U8, name="w1s", align_bytes=64)
-        w2s = keep.tile([128, E * N], U8, name="w2s", align_bytes=64)
         nc.vector.memset(w1s[:].bitcast(I32), 0)
-        nc.vector.memset(w2s[:].bitcast(I32), 0)
         ident = keep.tile([128, 128], F32, name="ident")
         make_identity(nc, ident[:])
         y = []
@@ -77,114 +84,124 @@ def tile_moe_cap2_mlp_silu_kernel(tc, xT, w1_words, w1_scales, w2_words, w2_scal
             nc.vector.memset(yb[:, S:], 0.0)
             y.append(yb)
 
+        w1w = {}
+
+        for e in range(2):
+            w = keep.tile([128, PASSES * 2 * H], U8, name=f"w1w_{e}", align_bytes=64)
+            w1w[e] = w[:]
+
+        def load_w1(e):
+            nc.sync.dma_start(
+                w1w[e].bitcast(I32).rearrange("p (s i) -> p s i", s=PASSES),
+                w1_words[e].bitcast(I32).rearrange("s p i -> p s i"),
+            )
+
+        load_w1(0)
         for Q in range(4):
             nc.sync.dma_start(
                 w1s[32 * Q : 32 * Q + 4, :].bitcast(I32).rearrange("p (g i) -> p g i", g=E * PASSES),
                 w1_scales[:, :, 4 * Q : 4 * Q + 4, :].bitcast(I32).rearrange("e s q i -> q (e s) i"),
             )
-        for Q in range(4):
-            nc.sync.dma_start(
-                w2s[32 * Q : 32 * Q + 4, :].bitcast(I32).rearrange("p (g i) -> p g i", g=E),
-                w2_scales[:, 0, 4 * Q : 4 * Q + 4, :].bitcast(I32).rearrange("e q i -> q e i"),
-            )
-        w1w = []
-        for e in range(E):
-            w = keep.tile([128, PASSES * 2 * H], U8, name=f"w1w_{e}", align_bytes=64)
-            nc.sync.dma_start(
-                w[:].bitcast(I32).rearrange("p (s i) -> p s i", s=PASSES),
-                w1_words[e].bitcast(I32).rearrange("s p i -> p s i"),
-            )
-            w1w.append(w)
-        w2w = keep.tile([128, E * 2 * N], U8, name="w2w", align_bytes=64)
-        nc.sync.dma_start(
-            w2w[:].bitcast(I32).rearrange("p (e i) -> p e i", e=E),
-            w2_words[:, 0].bitcast(I32).rearrange("e p i -> p e i"),
-        )
+        load_w1(1)
         nc.sync.dma_start(pos1_t[:], pos1)
         nc.sync.dma_start(pos2_t[:], pos2)
-        gates = []
-        for r in range(2):
-            g = keep.tile([128, T], F32, name=f"gate_{r}")
-            nc.sync.dma_start(g[:], gate[r, 0:128, :])
-            gates.append(g)
 
-        codes, slot_codes, slot_scales = [], [], []
+        codes, slot_codes = [], []
         for s in range(PASSES):
             c = keep.tile([128, T], U32, name=f"tok_codes_{s}", align_bytes=64)
             sc = keep.tile([128, S], U32, name=f"slot_codes_{s}", align_bytes=64)
-            ss = keep.tile([128, S], U8, name=f"slot_scales_{s}", align_bytes=64)
             codes.append(c)
             slot_codes.append(sc)
-            slot_scales.append(ss)
-
-        def cast(engine, s, lo, w, a, b, grouped):
-            dst = grouped[:, 4 * a : 4 * b].rearrange("p (c i t) -> p c t i", i=4, t=4)
-            src = raw[s, lo][:, :, a - lo : b - lo].rearrange("p t (c i) -> p c t i", i=4)
-            if engine == "v":
-                nc.vector.tensor_copy(dst, src)
-            else:
-                nc.scalar.activation(dst, src, COPY)
+        packed = keep.tile([128, S], U8, name="packed", align_bytes=64)
+        late = keep.tile([128, S], U8, name="late", align_bytes=64)
+        slot_scales = [packed, moved, late]
 
         def load_pass(s):
-            grouped = keep.tile([128, 4 * T], BF16, name=f"grouped_{s}", align_bytes=64)
-            if s == 0:
-                cast("s", 0, 0, 256, 0, 96, grouped)
-                cast("v", 0, 0, 256, 96, 256, grouped)
-                cast("s", 0, 256, 384, 256, 384, grouped)
-                cast("v", 0, 256, 384, 384, 640, grouped)
-            else:
-                cast("s", s, 0, 640, 0, 320, grouped)
-                cast("s", s, 0, 640, 320, 640, grouped)
-            for lo, w in quant[s]:
+            pool = turns if s == 2 else keep
+            grouped = pool.tile([128, 4 * T], BF16, name=f"grouped_{s}", tag=f"grouped_{s}", align_bytes=64)
+            for a, w, engine in CASTS[s]:
+                lo = max(c for c, n in CHUNKS if c <= a)
+                dst = grouped[:, 4 * a : 4 * (a + w)].rearrange("p (c i t) -> p c t i", i=4, t=4)
+                src = raw[s, lo][:, :, a - lo : a - lo + w].rearrange("p t (c i) -> p c t i", i=4)
+                if engine == "v":
+                    nc.vector.tensor_copy(dst, src)
+                else:
+                    nc.scalar.activation(dst, src, COPY)
+            for lo, w in QUANT:
                 nc.vector.quantize_mx(
                     out=codes[s][:, lo : lo + w].bitcast(FP8X4),
-                    scales=tok_scales[s][:, lo : lo + w],
+                    scales=tok_scales[0][4 * s :, lo : lo + w] if s < 2 else tok_scales[1][:, lo : lo + w],
                     in_=grouped[:, 4 * lo : 4 * (lo + w)],
                 )
 
-        def gather(s, lo, w):
+        def gather_words(s, lo, w):
             ids = offs_t[:, lo // 16 : (lo + w) // 16]
             nc.vector.tensor_copy(slot_codes[s][:, lo : lo + w], codes[s][:].indirect(ids))
-            nc.vector.tensor_copy(slot_scales[s][:, lo : lo + w], tok_scales[s][:].indirect(ids))
 
-        def layer1(m):
-            e = m // 2
-            cols = slice(128 * m, 128 * (m + 1))
-            acc = pacc.tile([128, H], F32, name="acc")
-            for s in range(PASSES):
-                nc.tensor.matmul_mx(
-                    out=acc[:],
-                    lhsT=slot_codes[s][:, cols].bitcast(FP8X4),
-                    lhsT_scale=slot_scales[s][:, cols],
-                    rhs=w1w[e][:, 2 * H * s : 2 * H * (s + 1)].bitcast(FP4X4),
-                    rhs_scale=w1s[:, H * (PASSES * e + s) : H * (PASSES * e + s + 1)],
-                    start=(s == 0),
-                    stop=(s == PASSES - 1),
+        def gather_bytes(dst, src, lo, w):
+            ids = offs_t[:, lo // 16 : (lo + w) // 16]
+            nc.vector.tensor_copy(dst[:, lo : lo + w], src[:].indirect(ids))
+
+        def gather_01(lo, w):
+            gather_bytes(packed, tok_scales[0], lo, w)
+            nc.scalar.dma_start(moved[0:112, lo : lo + w].bitcast(I32), packed[4:116, lo : lo + w].bitcast(I32))
+
+        def gather_2(lo, w):
+            gather_words(2, lo, w)
+            gather_bytes(late, tok_scales[1], lo, w)
+
+        hidden, grouped_h = {}, {}
+
+        def layer1(lo, w):
+            hg = keep.tile([128, 4 * w], BF16, name=f"hg_{lo}", align_bytes=64)
+            grouped_h[lo] = hg
+            for m in range(lo // 128, (lo + w) // 128):
+                e = m // 2
+                cols = slice(128 * m, 128 * (m + 1))
+                acc = pacc.tile([128, H], F32, name="acc")
+                for s in range(PASSES):
+                    nc.tensor.matmul_mx(
+                        out=acc[:],
+                        lhsT=slot_codes[s][:, cols].bitcast(FP8X4),
+                        lhsT_scale=slot_scales[s][:, cols],
+                        rhs=w1w[e][:, 2 * H * s : 2 * H * (s + 1)].bitcast(FP4X4),
+                        rhs_scale=w1s[:, H * (PASSES * e + s) : H * (PASSES * e + s + 1)],
+                        start=(s == 0),
+                        stop=(s == PASSES - 1),
+                    )
+                h = keep.tile([128, H], BF16, name=f"h_{m}", align_bytes=64)
+                nc.scalar.activation(
+                    h[:].rearrange("p (u q d) -> p u q d", u=2, d=2),
+                    acc[:].rearrange("p (q u d) -> p u q d", u=2, d=2),
+                    SILU,
                 )
-            h = keep.tile([128, H], BF16, name=f"h_{m}", align_bytes=64)
-            nc.scalar.activation(
-                h[:].rearrange("p (u q d) -> p u q d", u=2, d=2),
-                acc[:].rearrange("p (q u d) -> p u q d", u=2, d=2),
-                SILU,
-            )
-            return h
+                hidden[m] = h
 
-        def turn(h, hg, at):
-            words = h[:].bitcast(F32)
-            tp = ptr.tile([128, 2, 128], F32, name="tp")
-            for u in range(2):
-                nc.tensor.transpose(tp[:, u, :], words[:, 128 * u : 128 * (u + 1)], ident[:])
-            nc.scalar.copy(
-                hg[:, 4 * at : 4 * (at + 128)].bitcast(F32).rearrange("p (r u) -> p r u", u=2),
-                tp[:].rearrange("p u r -> p r u"),
-            )
+        def turn(lo, w):
+            for m in range(lo // 128, (lo + w) // 128):
+                at = 128 * m - lo
+                words = hidden[m][:].bitcast(F32)
+                tp = ptr.tile([128, 2, 128], F32, name="tp")
+                for u in range(2):
+                    nc.tensor.transpose(tp[:, u, :], words[:, 128 * u : 128 * (u + 1)], ident[:])
+                dst = grouped_h[lo][:, 4 * at : 4 * (at + 128)].bitcast(F32).rearrange("p (r u) -> p r u", u=2)
+                src = tp[:].rearrange("p u r -> p r u")
+                if TURN[m] == "v":
+                    nc.vector.tensor_copy(dst, src)
+                else:
+                    nc.scalar.copy(dst, src)
 
-        def layer2(unit, hg):
-            lo, w = unit
-            e = lo // C
+        quantised_h = {}
+
+        def quantise_h(lo, w):
             hc = keep.tile([128, w], U32, name=f"hc_{lo}", align_bytes=64)
             hs = keep.tile([128, w], U8, name=f"hs_{lo}", align_bytes=64)
-            nc.vector.quantize_mx(out=hc[:].bitcast(FP8X4), scales=hs[:], in_=hg[:])
+            nc.vector.quantize_mx(out=hc[:].bitcast(FP8X4), scales=hs[:], in_=grouped_h[lo][:])
+            quantised_h[lo] = (hc, hs)
+
+        def layer2(lo, w):
+            e = lo // C
+            hc, hs = quantised_h[lo]
             for b in range(NB):
                 p = py.tile([128, w], F32, name="p")
                 nc.tensor.matmul_mx(
@@ -196,40 +213,80 @@ def tile_moe_cap2_mlp_silu_kernel(tc, xT, w1_words, w1_scales, w2_words, w2_scal
                     start=True,
                     stop=True,
                 )
-                nc.scalar.copy(y[b][:, lo : lo + w], p[:])
+                if YCOPY.get((lo, b), "s") == "v":
+                    nc.vector.tensor_copy(y[b][:, lo : lo + w], p[:])
+                else:
+                    nc.scalar.copy(y[b][:, lo : lo + w], p[:])
 
-        for s in range(PASSES - 1):
-            load_pass(s)
-            for lo, w in CUTS:
-                gather(s, lo, w)
-        load_pass(PASSES - 1)
+        load_pass(0)
+        gather_words(0, 0, 384)
+        gather_words(0, 384, 384)
+        gather_words(0, 768, 256)
+        load_pass(1)
+        gather_01(0, 256)
+        gather_words(1, 0, 256)
+        gather_01(256, 256)
+        load_pass(2)
+        rest = turns.tile([128, 2 * PASSES * 2 * H], U8, name="rest", tag="raw_2_0", align_bytes=64)
+        for i in range(2):
+            w1w[2 + i] = rest[:, PASSES * 2 * H * i : PASSES * 2 * H * (i + 1)]
+        load_w1(2)
+        w2 = turns.tile([128, E * 3 * N], U8, name="w2", tag="raw_2_384", align_bytes=64)
+        w2w = w2[:, 0 : E * 2 * N]
+        w2s = w2[:, E * 2 * N :]
+        nc.gpsimd.memset(w2s.bitcast(I32), 0)
+        nc.sync.dma_start(
+            w2w.bitcast(I32).rearrange("p (e i) -> p e i", e=E),
+            w2_words[:, 0].bitcast(I32).rearrange("e p i -> p e i"),
+        )
+        for Q in range(4):
+            nc.sync.dma_start(
+                w2s[32 * Q : 32 * Q + 4, :].bitcast(I32).rearrange("p (g i) -> p g i", g=E),
+                w2_scales[:, 0, 4 * Q : 4 * Q + 4, :].bitcast(I32).rearrange("e q i -> q e i"),
+            )
+        load_w1(3)
+        both = turns.tile([128, 2, T], F32, name="both", tag="grouped_2", align_bytes=64)
+        nc.sync.dma_start(both[:], gate[:, 0:128, :].rearrange("r p t -> p r t"))
 
-        pending = None
-        for unit in UNITS:
-            lo, w = unit
-            gather(PASSES - 1, lo, w)
-            hg = keep.tile([128, 4 * w], BF16, name=f"hg_{lo}", align_bytes=64)
-            hs_ = [layer1(m) for m in range(lo // 128, (lo + w) // 128)]
-            if pending is not None:
-                layer2(*pending)
-            for i, h in enumerate(hs_):
-                turn(h, hg, 128 * i)
-            pending = (unit, hg)
-        layer2(*pending)
+        gather_2(0, 256)
+        layer1(0, 256)
+        turn(0, 256)
+        quantise_h(0, 256)
+        gather_words(1, 256, 256)
+        gather_2(256, 256)
+        gather_01(512, 256)
+        gather_01(768, 256)
+        layer1(256, 256)
+        turn(256, 256)
+        quantise_h(256, 256)
+        gather_words(1, 512, 256)
+        gather_2(512, 256)
+        layer1(512, 256)
+        turn(512, 256)
+        quantise_h(512, 256)
+        gather_words(1, 768, 256)
+        for lo in (768, 896):
+            gather_2(lo, 128)
+            layer1(lo, 128)
+            turn(lo, 128)
+            quantise_h(lo, 128)
+        for lo, w in UNITS:
+            layer2(lo, w)
 
-        prods = {}
-        outs = {}
+        prods, sums = {}, {}
+        for b in range(NB):
+            for r in range(2):
+                prods[b, r] = keep.tile([128, T], F32, name=f"prod_{b}_{r}")
+            sums[b] = keep.tile([128, T], F32, name=f"sum_{b}")
 
-        def product(b, r):
-            t = keep.tile([128, T], F32, name=f"prod_{b}_{r}")
-            ids = (pos1_t, pos2_t)[r]
-            nc.vector.tensor_tensor(t[:], y[b][:].indirect(ids[:]), gates[r][:], MULT)
-            prods[b, r] = t
+        def product(b, r, lo=0, w=T):
+            ids = (pos1_t, pos2_t)[r][:, lo // 16 : (lo + w) // 16]
+            nc.vector.tensor_tensor(prods[b, r][:, lo : lo + w], y[b][:].indirect(ids), both[:, r, lo : lo + w], MULT)
 
-        def total(b):
-            o = keep.tile([128, T], F32, name=f"o_{b}")
-            nc.vector.tensor_tensor(o[:], prods[b, 0][:], prods[b, 1][:], ADD)
-            nc.sync.dma_start(out[128 * b : 128 * (b + 1), :], o[:])
+        def total(b, lo=0, w=T):
+            cols = slice(lo, lo + w)
+            nc.vector.tensor_tensor(sums[b][:, cols], prods[b, 0][:, cols], prods[b, 1][:, cols], ADD)
+            nc.sync.dma_start(out[128 * b : 128 * (b + 1), cols], sums[b][:, cols])
 
         product(0, 0)
         product(0, 1)
@@ -238,5 +295,7 @@ def tile_moe_cap2_mlp_silu_kernel(tc, xT, w1_words, w1_scales, w2_words, w2_scal
         product(1, 1)
         product(2, 0)
         total(1)
-        product(2, 1)
-        total(2)
+        product(2, 1, 0, 320)
+        product(2, 1, 320, 320)
+        total(2, 0, 320)
+        total(2, 320, 320)

@@ -34,7 +34,8 @@ CASTS = [
 UNITS = [(0, 256), (256, 256), (512, 256), (768, 128), (896, 128)]
 QUANT = [(0, 256), (256, 128), (384, 256)]
 TURN = "ssssvvvv"
-YCOPY = {(0, 1): "v", (256, 1): "v", (512, 1): "v", (768, 1): "v"}
+YCOPY = {(0, 1): "v", (256, 1): "v"}
+WIN = T + 64
 
 
 def tile_moe_cap2_mlp_silu_kernel(tc, xT, w1_words, w1_scales, w2_words, w2_scales, gate, offs, pos1, pos2, out):
@@ -43,9 +44,9 @@ def tile_moe_cap2_mlp_silu_kernel(tc, xT, w1_words, w1_scales, w2_words, w2_scal
         lists = ctx.enter_context(tc.tile_pool(name="lists", bufs=1))
         keep = ctx.enter_context(tc.tile_pool(name="keep", bufs=1))
         turns = ctx.enter_context(tc.tile_pool(name="turns", bufs=1))
-        pacc = ctx.enter_context(tc.psum_pool(name="pacc", bufs=3))
+        pacc = ctx.enter_context(tc.psum_pool(name="pacc", bufs=4))
         ptr = ctx.enter_context(tc.psum_pool(name="ptr", bufs=2))
-        py = ctx.enter_context(tc.psum_pool(name="py", bufs=3))
+        py = ctx.enter_context(tc.psum_pool(name="py", bufs=2))
 
         offs_t = lists.tile([128, S // 16], U16, name="offs_t")
         pos1_t = lists.tile([128, T // 16], U16, name="pos1_t")
@@ -61,6 +62,8 @@ def tile_moe_cap2_mlp_silu_kernel(tc, xT, w1_words, w1_scales, w2_words, w2_scal
                 raw[s, lo] = r
             if s == 0:
                 nc.sync.dma_start(offs_t[:], offs)
+                nc.sync.dma_start(pos1_t[:], pos1)
+                nc.sync.dma_start(pos2_t[:], pos2)
 
         warm = keep.tile([128, 1], F32, name="warm")
         warm_out = keep.tile([128, 1], F32, name="warm_out")
@@ -69,7 +72,7 @@ def tile_moe_cap2_mlp_silu_kernel(tc, xT, w1_words, w1_scales, w2_words, w2_scal
 
         tok_scales = []
         for s in range(2):
-            z = keep.tile([128, T], U8, name=f"tok_scales_{s}", align_bytes=64)
+            z = keep.tile([128, WIN], U8, name=f"tok_scales_{s}", align_bytes=64)
             nc.gpsimd.memset(z[:], 0)
             tok_scales.append(z)
         moved = keep.tile([128, S], U8, name="moved", align_bytes=64)
@@ -103,12 +106,11 @@ def tile_moe_cap2_mlp_silu_kernel(tc, xT, w1_words, w1_scales, w2_words, w2_scal
                 w1_scales[:, :, 4 * Q : 4 * Q + 4, :].bitcast(I32).rearrange("e s q i -> q (e s) i"),
             )
         load_w1(1)
-        nc.sync.dma_start(pos1_t[:], pos1)
-        nc.sync.dma_start(pos2_t[:], pos2)
 
         codes, slot_codes = [], []
         for s in range(PASSES):
-            c = keep.tile([128, T], U32, name=f"tok_codes_{s}", align_bytes=64)
+            c = keep.tile([128, WIN], I32, name=f"tok_codes_{s}", align_bytes=64)
+            nc.vector.memset(c[:, T:], 0)
             sc = keep.tile([128, S], U32, name=f"slot_codes_{s}", align_bytes=64)
             codes.append(c)
             slot_codes.append(sc)
@@ -136,7 +138,7 @@ def tile_moe_cap2_mlp_silu_kernel(tc, xT, w1_words, w1_scales, w2_words, w2_scal
 
         def gather_words(s, lo, w):
             ids = offs_t[:, lo // 16 : (lo + w) // 16]
-            nc.vector.tensor_copy(slot_codes[s][:, lo : lo + w], codes[s][:].indirect(ids))
+            nc.vector.tensor_copy(slot_codes[s][:, lo : lo + w], codes[s][:].bitcast(U32).indirect(ids))
 
         def gather_bytes(dst, src, lo, w):
             ids = offs_t[:, lo // 16 : (lo + w) // 16]
@@ -199,29 +201,27 @@ def tile_moe_cap2_mlp_silu_kernel(tc, xT, w1_words, w1_scales, w2_words, w2_scal
             nc.vector.quantize_mx(out=hc[:].bitcast(FP8X4), scales=hs[:], in_=grouped_h[lo][:])
             quantised_h[lo] = (hc, hs)
 
-        def layer2(lo, w):
+        def layer2(lo, w, b):
             e = lo // C
             hc, hs = quantised_h[lo]
-            for b in range(NB):
-                p = py.tile([128, w], F32, name="p")
-                nc.tensor.matmul_mx(
-                    out=p[:],
-                    lhsT=w2w[:, 2 * (N * e + 128 * b) : 2 * (N * e + 128 * (b + 1))].bitcast(FP4X4),
-                    lhsT_scale=w2s[:, N * e + 128 * b : N * e + 128 * (b + 1)],
-                    rhs=hc[:].bitcast(FP8X4),
-                    rhs_scale=hs[:],
-                    start=True,
-                    stop=True,
-                )
-                if YCOPY.get((lo, b), "s") == "v":
-                    nc.vector.tensor_copy(y[b][:, lo : lo + w], p[:])
-                else:
-                    nc.scalar.copy(y[b][:, lo : lo + w], p[:])
+            p = py.tile([128, w], F32, name="p")
+            nc.tensor.matmul_mx(
+                out=p[:],
+                lhsT=w2w[:, 2 * (N * e + 128 * b) : 2 * (N * e + 128 * (b + 1))].bitcast(FP4X4),
+                lhsT_scale=w2s[:, N * e + 128 * b : N * e + 128 * (b + 1)],
+                rhs=hc[:].bitcast(FP8X4),
+                rhs_scale=hs[:],
+                start=True,
+                stop=True,
+            )
+            if YCOPY.get((lo, b), "s") == "v":
+                nc.vector.tensor_copy(y[b][:, lo : lo + w], p[:])
+            else:
+                nc.scalar.copy(y[b][:, lo : lo + w], p[:])
 
         load_pass(0)
-        gather_words(0, 0, 384)
-        gather_words(0, 384, 384)
-        gather_words(0, 768, 256)
+        gather_words(0, 0, 512)
+        gather_words(0, 512, 512)
         load_pass(1)
         gather_01(0, 256)
         gather_words(1, 0, 256)
@@ -248,30 +248,30 @@ def tile_moe_cap2_mlp_silu_kernel(tc, xT, w1_words, w1_scales, w2_words, w2_scal
         both = turns.tile([128, 2, T], F32, name="both", tag="grouped_2", align_bytes=64)
         nc.sync.dma_start(both[:], gate[:, 0:128, :].rearrange("r p t -> p r t"))
 
+        def unit(lo, w):
+            layer1(lo, w)
+            turn(lo, w)
+            quantise_h(lo, w)
+
         gather_2(0, 256)
-        layer1(0, 256)
-        turn(0, 256)
-        quantise_h(0, 256)
+        unit(0, 256)
         gather_words(1, 256, 256)
         gather_2(256, 256)
-        gather_01(512, 256)
-        gather_01(768, 256)
-        layer1(256, 256)
-        turn(256, 256)
-        quantise_h(256, 256)
-        gather_words(1, 512, 256)
+        gather_01(512, 512)
+        unit(256, 256)
+        gather_words(1, 512, 512)
         gather_2(512, 256)
-        layer1(512, 256)
-        turn(512, 256)
-        quantise_h(512, 256)
-        gather_words(1, 768, 256)
+        unit(512, 256)
+        gather_words(2, 768, 256)
         for lo in (768, 896):
-            gather_2(lo, 128)
-            layer1(lo, 128)
-            turn(lo, 128)
-            quantise_h(lo, 128)
-        for lo, w in UNITS:
-            layer2(lo, w)
+            gather_bytes(late, tok_scales[1], lo, 128)
+            unit(lo, 128)
+        for lo, w in UNITS[:2]:
+            for b in range(NB):
+                layer2(lo, w, b)
+        for b in range(NB):
+            for lo, w in UNITS[2:]:
+                layer2(lo, w, b)
 
         prods, sums = {}, {}
         for b in range(NB):

from contextlib import ExitStack

import concourse.mybir as mybir
from concourse.masks import make_identity

K, T, E, C, H, N = 1536, 640, 4, 256, 512, 384
PAD = 32
S = E * C
PASSES = K // 512
NB = N // 128

FLOPS = 2 * S * H * (K + N)
BYTES = 4 * K * T + E * K * H // 2 + E * K * H // 32 + E * H * N // 2 + E * H * N // 32 + 2 * 4 * T + 2 * (S + 2 * T) + 4 * N * T

F32 = mybir.dt.float32
BF16 = mybir.dt.bfloat16
U32 = mybir.dt.uint32
I32 = mybir.dt.int32
U16 = mybir.dt.uint16
U8 = mybir.dt.uint8
FP8X4 = mybir.dt.float8_e4m3fn_x4
FP4X4 = mybir.dt.float4_e2m1fn_x4
COPY = mybir.ActivationFunctionType.Copy
SILU = mybir.ActivationFunctionType.Silu
MULT = mybir.AluOpType.mult
ADD = mybir.AluOpType.add

CHUNKS = [(0, 384), (384, 256)]
CASTS = [
    [(0, 160, "s"), (160, 224, "v"), (384, 96, "s"), (480, 160, "v")],
    [(0, 384, "s"), (384, 160, "s"), (544, 96, "v")],
    [(0, 384, "s"), (384, 256, "s")],
]
UNITS = [(0, 256), (256, 256), (512, 256), (768, 128), (896, 128)]
QUANT = [(0, 256), (256, 128), (384, 256)]
TURN = "ssssvvvv"
YCOPY = {(0, 1): "v", (256, 1): "v"}
WIN = T + 64


def tile_moe_cap2_mlp_silu_kernel(tc, xT, w1_words, w1_scales, w2_words, w2_scales, gate, offs, pos1, pos2, out):
    nc = tc.nc
    with ExitStack() as ctx:
        lists = ctx.enter_context(tc.tile_pool(name="lists", bufs=1))
        keep = ctx.enter_context(tc.tile_pool(name="keep", bufs=1))
        turns = ctx.enter_context(tc.tile_pool(name="turns", bufs=1))
        pacc = ctx.enter_context(tc.psum_pool(name="pacc", bufs=4))
        ptr = ctx.enter_context(tc.psum_pool(name="ptr", bufs=2))
        py = ctx.enter_context(tc.psum_pool(name="py", bufs=2))

        offs_t = lists.tile([128, S // 16], U16, name="offs_t")
        pos1_t = lists.tile([128, T // 16], U16, name="pos1_t")
        pos2_t = lists.tile([128, T // 16], U16, name="pos2_t")

        raw = {}
        for s in range(PASSES):
            rows = xT[512 * s : 512 * (s + 1), :].rearrange("(p j) t -> p j t", j=4)
            for lo, w in CHUNKS:
                pool = turns if s == 2 else keep
                r = pool.tile([128, 4, w], F32, name=f"raw_{s}_{lo}", tag=f"raw_{s}_{lo}", align_bytes=64)
                nc.sync.dma_start(r[:], rows[:, :, lo : lo + w])
                raw[s, lo] = r
            if s == 0:
                nc.sync.dma_start(offs_t[:], offs)
                nc.sync.dma_start(pos1_t[:], pos1)
                nc.sync.dma_start(pos2_t[:], pos2)

        warm = keep.tile([128, 1], F32, name="warm")
        warm_out = keep.tile([128, 1], F32, name="warm_out")
        nc.vector.memset(warm[:], 0.0)
        nc.scalar.activation(warm_out[:], warm[:], SILU)

        tok_scales = []
        for s in range(2):
            z = keep.tile([128, WIN], U8, name=f"tok_scales_{s}", align_bytes=64)
            nc.gpsimd.memset(z[:], 0)
            tok_scales.append(z)
        moved = keep.tile([128, S], U8, name="moved", align_bytes=64)
        nc.gpsimd.memset(moved[:], 0)
        w1s = keep.tile([128, E * PASSES * H], U8, name="w1s", align_bytes=64)
        nc.vector.memset(w1s[:].bitcast(I32), 0)
        ident = keep.tile([128, 128], F32, name="ident")
        make_identity(nc, ident[:])
        y = []
        for b in range(NB):
            yb = keep.tile([128, S + PAD], F32, name=f"y_{b}", align_bytes=64)
            nc.vector.memset(yb[:, S:], 0.0)
            y.append(yb)

        w1w = {}

        for e in range(2):
            w = keep.tile([128, PASSES * 2 * H], U8, name=f"w1w_{e}", align_bytes=64)
            w1w[e] = w[:]

        def load_w1(e):
            nc.sync.dma_start(
                w1w[e].bitcast(I32).rearrange("p (s i) -> p s i", s=PASSES),
                w1_words[e].bitcast(I32).rearrange("s p i -> p s i"),
            )

        load_w1(0)
        for Q in range(4):
            nc.sync.dma_start(
                w1s[32 * Q : 32 * Q + 4, :].bitcast(I32).rearrange("p (g i) -> p g i", g=E * PASSES),
                w1_scales[:, :, 4 * Q : 4 * Q + 4, :].bitcast(I32).rearrange("e s q i -> q (e s) i"),
            )
        load_w1(1)

        codes, slot_codes = [], []
        for s in range(PASSES):
            c = keep.tile([128, WIN], I32, name=f"tok_codes_{s}", align_bytes=64)
            nc.vector.memset(c[:, T:], 0)
            sc = keep.tile([128, S], U32, name=f"slot_codes_{s}", align_bytes=64)
            codes.append(c)
            slot_codes.append(sc)
        packed = keep.tile([128, S], U8, name="packed", align_bytes=64)
        late = keep.tile([128, S], U8, name="late", align_bytes=64)
        slot_scales = [packed, moved, late]

        def load_pass(s):
            pool = turns if s == 2 else keep
            grouped = pool.tile([128, 4 * T], BF16, name=f"grouped_{s}", tag=f"grouped_{s}", align_bytes=64)
            for a, w, engine in CASTS[s]:
                lo = max(c for c, n in CHUNKS if c <= a)
                dst = grouped[:, 4 * a : 4 * (a + w)].rearrange("p (c i t) -> p c t i", i=4, t=4)
                src = raw[s, lo][:, :, a - lo : a - lo + w].rearrange("p t (c i) -> p c t i", i=4)
                if engine == "v":
                    nc.vector.tensor_copy(dst, src)
                else:
                    nc.scalar.activation(dst, src, COPY)
            for lo, w in QUANT:
                nc.vector.quantize_mx(
                    out=codes[s][:, lo : lo + w].bitcast(FP8X4),
                    scales=tok_scales[0][4 * s :, lo : lo + w] if s < 2 else tok_scales[1][:, lo : lo + w],
                    in_=grouped[:, 4 * lo : 4 * (lo + w)],
                )

        def gather_words(s, lo, w):
            ids = offs_t[:, lo // 16 : (lo + w) // 16]
            nc.vector.tensor_copy(slot_codes[s][:, lo : lo + w], codes[s][:].bitcast(U32).indirect(ids))

        def gather_bytes(dst, src, lo, w):
            ids = offs_t[:, lo // 16 : (lo + w) // 16]
            nc.vector.tensor_copy(dst[:, lo : lo + w], src[:].indirect(ids))

        def gather_01(lo, w):
            gather_bytes(packed, tok_scales[0], lo, w)
            nc.scalar.dma_start(moved[0:112, lo : lo + w].bitcast(I32), packed[4:116, lo : lo + w].bitcast(I32))

        def gather_2(lo, w):
            gather_words(2, lo, w)
            gather_bytes(late, tok_scales[1], lo, w)

        hidden, grouped_h = {}, {}

        def layer1(lo, w):
            hg = keep.tile([128, 4 * w], BF16, name=f"hg_{lo}", align_bytes=64)
            grouped_h[lo] = hg
            for m in range(lo // 128, (lo + w) // 128):
                e = m // 2
                cols = slice(128 * m, 128 * (m + 1))
                acc = pacc.tile([128, H], F32, name="acc")
                for s in range(PASSES):
                    nc.tensor.matmul_mx(
                        out=acc[:],
                        lhsT=slot_codes[s][:, cols].bitcast(FP8X4),
                        lhsT_scale=slot_scales[s][:, cols],
                        rhs=w1w[e][:, 2 * H * s : 2 * H * (s + 1)].bitcast(FP4X4),
                        rhs_scale=w1s[:, H * (PASSES * e + s) : H * (PASSES * e + s + 1)],
                        start=(s == 0),
                        stop=(s == PASSES - 1),
                    )
                h = keep.tile([128, H], BF16, name=f"h_{m}", align_bytes=64)
                nc.scalar.activation(
                    h[:].rearrange("p (u q d) -> p u q d", u=2, d=2),
                    acc[:].rearrange("p (q u d) -> p u q d", u=2, d=2),
                    SILU,
                )
                hidden[m] = h

        def turn(lo, w):
            for m in range(lo // 128, (lo + w) // 128):
                at = 128 * m - lo
                words = hidden[m][:].bitcast(F32)
                tp = ptr.tile([128, 2, 128], F32, name="tp")
                for u in range(2):
                    nc.tensor.transpose(tp[:, u, :], words[:, 128 * u : 128 * (u + 1)], ident[:])
                dst = grouped_h[lo][:, 4 * at : 4 * (at + 128)].bitcast(F32).rearrange("p (r u) -> p r u", u=2)
                src = tp[:].rearrange("p u r -> p r u")
                if TURN[m] == "v":
                    nc.vector.tensor_copy(dst, src)
                else:
                    nc.scalar.copy(dst, src)

        quantised_h = {}

        def quantise_h(lo, w):
            hc = keep.tile([128, w], U32, name=f"hc_{lo}", align_bytes=64)
            hs = keep.tile([128, w], U8, name=f"hs_{lo}", align_bytes=64)
            nc.vector.quantize_mx(out=hc[:].bitcast(FP8X4), scales=hs[:], in_=grouped_h[lo][:])
            quantised_h[lo] = (hc, hs)

        def layer2(lo, w, b):
            e = lo // C
            hc, hs = quantised_h[lo]
            p = py.tile([128, w], F32, name="p")
            nc.tensor.matmul_mx(
                out=p[:],
                lhsT=w2w[:, 2 * (N * e + 128 * b) : 2 * (N * e + 128 * (b + 1))].bitcast(FP4X4),
                lhsT_scale=w2s[:, N * e + 128 * b : N * e + 128 * (b + 1)],
                rhs=hc[:].bitcast(FP8X4),
                rhs_scale=hs[:],
                start=True,
                stop=True,
            )
            if YCOPY.get((lo, b), "s") == "v":
                nc.vector.tensor_copy(y[b][:, lo : lo + w], p[:])
            else:
                nc.scalar.copy(y[b][:, lo : lo + w], p[:])

        load_pass(0)
        gather_words(0, 0, 512)
        gather_words(0, 512, 512)
        load_pass(1)
        gather_01(0, 256)
        gather_words(1, 0, 256)
        gather_01(256, 256)
        load_pass(2)
        rest = turns.tile([128, 2 * PASSES * 2 * H], U8, name="rest", tag="raw_2_0", align_bytes=64)
        for i in range(2):
            w1w[2 + i] = rest[:, PASSES * 2 * H * i : PASSES * 2 * H * (i + 1)]
        load_w1(2)
        w2 = turns.tile([128, E * 3 * N], U8, name="w2", tag="raw_2_384", align_bytes=64)
        w2w = w2[:, 0 : E * 2 * N]
        w2s = w2[:, E * 2 * N :]
        nc.gpsimd.memset(w2s.bitcast(I32), 0)
        nc.sync.dma_start(
            w2w.bitcast(I32).rearrange("p (e i) -> p e i", e=E),
            w2_words[:, 0].bitcast(I32).rearrange("e p i -> p e i"),
        )
        for Q in range(4):
            nc.sync.dma_start(
                w2s[32 * Q : 32 * Q + 4, :].bitcast(I32).rearrange("p (g i) -> p g i", g=E),
                w2_scales[:, 0, 4 * Q : 4 * Q + 4, :].bitcast(I32).rearrange("e q i -> q e i"),
            )
        load_w1(3)
        both = turns.tile([128, 2, T], F32, name="both", tag="grouped_2", align_bytes=64)
        nc.sync.dma_start(both[:], gate[:, 0:128, :].rearrange("r p t -> p r t"))

        def unit(lo, w):
            layer1(lo, w)
            turn(lo, w)
            quantise_h(lo, w)

        gather_2(0, 256)
        unit(0, 256)
        gather_words(1, 256, 256)
        gather_2(256, 256)
        gather_01(512, 512)
        unit(256, 256)
        gather_words(1, 512, 512)
        gather_2(512, 256)
        unit(512, 256)
        gather_words(2, 768, 256)
        for lo in (768, 896):
            gather_bytes(late, tok_scales[1], lo, 128)
            unit(lo, 128)
        for lo, w in UNITS[:2]:
            for b in range(NB):
                layer2(lo, w, b)
        for b in range(NB):
            for lo, w in UNITS[2:]:
                layer2(lo, w, b)

        prods, sums = {}, {}
        for b in range(NB):
            for r in range(2):
                prods[b, r] = keep.tile([128, T], F32, name=f"prod_{b}_{r}")
            sums[b] = keep.tile([128, T], F32, name=f"sum_{b}")

        def product(b, r, lo=0, w=T):
            ids = (pos1_t, pos2_t)[r][:, lo // 16 : (lo + w) // 16]
            nc.vector.tensor_tensor(prods[b, r][:, lo : lo + w], y[b][:].indirect(ids), both[:, r, lo : lo + w], MULT)

        def total(b, lo=0, w=T):
            cols = slice(lo, lo + w)
            nc.vector.tensor_tensor(sums[b][:, cols], prods[b, 0][:, cols], prods[b, 1][:, cols], ADD)
            nc.sync.dma_start(out[128 * b : 128 * (b + 1), cols], sums[b][:, cols])

        product(0, 0)
        product(0, 1)
        product(1, 0)
        total(0)
        product(1, 1)
        product(2, 0)
        total(1)
        product(2, 1, 0, 320)
        product(2, 1, 320, 320)
        total(2, 0, 320)
        total(2, 320, 320)
